import numpy as np
import ml_dtypes


def mxq(x, axis, fmt="e4m3"):
    dtype, down = {"e4m3": (ml_dtypes.float8_e4m3fn, 7), "e5m2": (ml_dtypes.float8_e5m2, 14)}[fmt]
    v = np.moveaxis(np.asarray(x, np.float32).astype(ml_dtypes.bfloat16).astype(np.float64), axis, -1)
    blocks = v.reshape(v.shape[:-1] + (-1, 32))
    amax = np.abs(blocks).max(-1, keepdims=True)
    byte = np.maximum(np.where(amax > 0, np.frexp(amax)[1] - 1 + 127, 0) - down, 1)
    scale = np.exp2(byte - 127.0)
    codes = (blocks / scale).astype(np.float32).astype(dtype).astype(np.float64)
    return np.moveaxis((codes * scale).reshape(v.shape), -1, axis)


WIDE = False


def mx_kscale(k):
    if not WIDE:
        return np.ones(k)
    levels = np.array([10, -10, 5, -5, 0])
    if k % 512:
        return np.exp2(np.random.permutation(np.resize(levels, k // 32))).repeat(32)
    a = np.empty((k // 512, 16))
    for p in range(k // 512):
        a[p, :8] = np.random.permutation(np.resize(levels, 8))
        for g in range(8):
            far = levels[np.abs(levels - a[p, g]) >= 10]
            a[p, g + 8] = far[np.random.randint(len(far))]
    return np.exp2(a.ravel()).repeat(32)


def f64(x):
    return np.asarray(x).astype(np.float64)


def striped(idx):
    return np.tile(idx.reshape(-1, 16).T, (8, 1)).astype(np.uint16)


def unstriped(offs):
    return offs[:16].T.reshape(-1).astype(np.int64)


def striped8(idx):
    return np.concatenate([x.reshape(-1, 16).T for x in idx]).astype(np.uint16)


def runs(offs, k):
    lists = np.stack([offs[16 * r : 16 * r + 16].T.reshape(-1) for r in range(8)]).astype(np.int64)
    return lists[np.arange(k) % 512 // 64]


def pack_weight(w):
    k, n = w.shape
    w = f64(np.asarray(w, np.float32).astype(ml_dtypes.bfloat16)).reshape(k // 32, 32, n)
    amax = np.abs(w).max(1)
    byte = np.clip(np.where(amax > 0, np.frexp(amax)[1] - 1 + 127 - 7, 1), 1, 254)
    scaled = (w * np.exp2(127.0 - byte)[:, None, :]).reshape(k, n).astype(np.float32)
    words = np.ascontiguousarray(scaled.reshape(k // 512, 128, 4, n).transpose(0, 1, 3, 2)).astype(ml_dtypes.float8_e4m3fn).view(np.uint8)
    return words, np.ascontiguousarray(byte.astype(np.uint8).reshape(k // 512, 16, n))


def unpack_weight(words, scales):
    g, p, n, _ = words.shape
    vals = np.ascontiguousarray(words).view(ml_dtypes.float8_e4m3fn).astype(np.float64) * np.repeat(np.exp2(scales.astype(np.float64) - 127.0), 8, axis=1)[..., None]
    return vals.transpose(0, 1, 3, 2).reshape(g * 512, n)

def planes(y):
    n, m = y.shape
    v = y.astype(np.float32).astype(ml_dtypes.bfloat16).astype(np.float64).reshape(n // 32, 32, m)
    top = np.abs(v).max(1)
    byte = np.clip(np.where(top > 0, np.frexp(top)[1] - 1 + 127 - 7, 1), 1, 254)
    codes = (v * np.exp2(127.0 - byte)[:, None, :]).reshape(n, m).astype(np.float32).astype(ml_dtypes.float8_e4m3fn).view(np.uint8)
    words = codes.reshape(n // 512, 128, 4, m).transpose(0, 1, 3, 2)
    return np.ascontiguousarray(words), np.ascontiguousarray(byte.astype(np.uint8).reshape(n // 512, 16, m))


K, T, S, H, C = 512, 2048, 256, 512, 512


def setup_inputs():
    n = np.random.standard_normal
    s = mx_kscale(K)[:, None]
    packed_xT = pack_weight(n((K, T)) * s)
    packed_w1 = pack_weight(n((K, H)) / np.sqrt(K) / s)
    return {
        "x_words": packed_xT[0],
        "x_scales": packed_xT[1],
        "w1_words": packed_w1[0],
        "w1_scales": packed_w1[1],
        "tau": np.random.uniform(0.3, 0.9, (H, 1)).astype(np.float32),
        "gs": (np.random.uniform(0.5, 1.5, (K, 1)) / s).astype(np.float32),
        "tau2": np.random.uniform(0.3, 0.9, (C, 1)).astype(np.float32),
        "offs": striped(np.random.permutation(T)[:S]),
        "n1": striped8(np.stack([np.random.permutation(S) for _ in range(8)])),
        "n2": striped8(np.stack([np.random.permutation(S) for _ in range(8)])),
        "ca": striped(np.random.permutation(T)[:C]),
        "cb": striped(np.random.permutation(T)[:C]),
        "n3": striped8(np.stack([np.random.permutation(S) for _ in range(8)])),
        "n4": striped8(np.stack([np.random.permutation(S) for _ in range(8)])),
    }


def reference(x_words, x_scales, w1_words, w1_scales, tau, gs, tau2, offs, n1, n2, ca, cb, n3, n4):
    x_ca = unpack_weight(x_words, x_scales)[:, unstriped(ca)]
    xq = unpack_weight(x_words, x_scales)[:, unstriped(offs)]
    y = unpack_weight(w1_words, w1_scales).T @ xq
    low = y.min(axis=1, keepdims=True)
    ea = np.exp(f64(tau) * (low - (y[np.arange(H)[:, None], runs(n1, H)])))
    z = f64(gs) * (y - (2.0 * (ea * (y[np.arange(H)[:, None], runs(n2, H)]))))
    zq = mxq(z, 0, "e4m3")
    a = 0.0625 * (x_ca.T @ zq)
    x_cb = unpack_weight(x_words, x_scales)[:, unstriped(cb)]
    b = 0.0625 * (x_cb.T @ zq)
    top = b.max(axis=1, keepdims=True)
    ea2 = np.exp(f64(tau2) * (b[np.arange(C)[:, None], runs(n3, C)] - top))
    out_0 = (0.5 * (a - (a[np.arange(C)[:, None], runs(n4, C)]))) / (ea2 + 0.25)
    return (out_0,) + planes(out_0)

@@ -1,0 +1,217 @@
+from contextlib import ExitStack
+
+import concourse.mybir as mybir
+
+K, T, S, H, C = 512, 2048, 256, 512, 512
+FLOPS = 2 * K * S * (H + 2 * C)
+
+F32 = mybir.dt.float32
+BF16 = mybir.dt.bfloat16
+I32 = mybir.dt.int32
+U32 = mybir.dt.uint32
+U16 = mybir.dt.uint16
+U8 = mybir.dt.uint8
+FP8X4 = mybir.dt.float8_e4m3fn_x4
+ALU = mybir.AluOpType
+ACT = mybir.ActivationFunctionType
+
+P = 128
+PACK = 4
+HALF = S // 2
+
+
+def tile_picked_ccmpqxbebz_none_po_kernel(tc, x_words, x_scales, w1_words, w1_scales, tau, gs, tau2, offs, n1, n2, ca, cb, n3, n4, out_0, out_1, out_2):
+    nc = tc.nc
+    with ExitStack() as ctx:
+        keep = ctx.enter_context(tc.tile_pool(name="keep", bufs=1))
+        psum = ctx.enter_context(tc.psum_pool(name="psum", bufs=1))
+
+        def sb(name, shape, dtype, tag=None):
+            return keep.tile(shape, dtype, name=name, tag=tag or name, align_bytes=64)
+
+        def load_list(name, src):
+            tile = sb(name, list(src.shape), U16)
+            nc.sync.dma_start(tile[:], src)
+            return tile
+
+        def load_column(name, src, queue):
+            tile = sb(name, [P, PACK], F32)
+            queue.dma_start(tile[:], src.rearrange("(p t) o -> p (t o)", t=PACK))
+            return tile
+
+        def load_scale_rows(tile, src, q, queue):
+            rows = src[0][4 * q : 4 * q + 4, :].bitcast(I32)
+            queue.dma_start(tile[32 * q : 32 * q + 32, :].bitcast(I32), rows.partition_broadcast(8))
+
+        xs = sb("xs", [P, T], U8)
+        for q in range(3):
+            load_scale_rows(xs, x_scales, q, nc.scalar)
+        offs_sb = load_list("offs_sb", offs)
+        cb_sb = load_list("cb_sb", cb)
+        ca_sb = load_list("ca_sb", ca)
+        load_scale_rows(xs, x_scales, 3, nc.sync)
+        xw = sb("xw", [P, T], U32)
+        nc.sync.dma_start(xw[:].bitcast(I32), x_words[0].rearrange("p n r -> p (n r)").bitcast(I32))
+        ws_raw = sb("ws_raw", [P, H], U8)
+        for q in range(4):
+            load_scale_rows(ws_raw, w1_scales, q, nc.sync)
+        ww_raw = sb("ww_raw", [P, H], U32)
+        nc.sync.dma_start(ww_raw[:].bitcast(I32), w1_words[0].rearrange("p n r -> p (n r)").bitcast(I32))
+        n2_sb = load_list("n2_sb", n2)
+        n1_sb = load_list("n1_sb", n1)
+        n3_sb = load_list("n3_sb", n3)
+        n4_sb = load_list("n4_sb", n4)
+        tau_sb = load_column("tau_sb", tau, nc.gpsimd)
+        gs_sb = load_column("gs_sb", gs, nc.gpsimd)
+        tau2_sb = load_column("tau2_sb", tau2, nc.gpsimd)
+
+        y_win = [sb("y_win%d" % t, [P, 2 * S], F32) for t in range(PACK)]
+        a_win = [sb("a_win%d" % t, [P, 2 * S], F32) for t in range(PACK)]
+        b_win = [sb("b_win%d" % t, [P, 2 * S], F32) for t in range(PACK)]
+        for t in range(PACK):
+            nc.vector.memset(y_win[t][:, S:], 0.0)
+
+        def dealt(ap):
+            return ap.rearrange("p (t m) -> p m t", t=PACK)
+
+        xq_s = sb("xq_s", [P, S], U8)
+        nc.vector.tensor_copy(xq_s[:], xs[:].indirect(offs_sb[:]))
+        cb_s = sb("cb_s", [P, C], U8)
+        nc.vector.tensor_copy(dealt(cb_s[:]), xs[:].indirect(cb_sb[:]))
+        ca_s = sb("ca_s", [P, C], U8)
+        nc.vector.tensor_copy(dealt(ca_s[:]), xs[:].indirect(ca_sb[:]))
+        w_s = sb("w_s", [P, H], U8)
+        nc.vector.tensor_copy(w_s[:].rearrange("p (t m) -> p t m", t=PACK), ws_raw[:].rearrange("p (m t) -> p t m", t=PACK))
+        neg_tau = sb("neg_tau", [P, PACK], F32)
+        nc.gpsimd.tensor_scalar(neg_tau[:], tau_sb[:], -1.0, 0.0, ALU.mult, ALU.add)
+        neg2_gs = sb("neg2_gs", [P, PACK], F32)
+        nc.gpsimd.tensor_scalar(neg2_gs[:], gs_sb[:], -2.0, 0.0, ALU.mult, ALU.add)
+
+        xq_w = sb("xq_w", [P, S], U32)
+        nc.vector.tensor_copy(xq_w[:], xw[:].indirect(offs_sb[:]))
+        w_w = sb("w_w", [P, H], U32)
+        for t in range(PACK):
+            nc.scalar.copy(w_w[:, P * t : P * (t + 1)], ww_raw[:, t:H:PACK])
+
+        def pick_half(lst, dst, h, name, tag=None):
+            picked = sb(name, [P, C // 2], U32, tag)
+            nc.vector.tensor_copy(picked[:], xw[:].indirect(lst[:, 16 * h : 16 * (h + 1)]))
+            nc.vector.tensor_copy(dealt(dst[:])[:, 64 * h : 64 * (h + 1), :], picked[:].rearrange("p (m t) -> p m t", t=PACK))
+
+        cb_w = sb("cb_w", [P, C], U32)
+        ca_w = sb("ca_w", [P, C], U32)
+        pick_half(cb_sb, cb_w, 0, "cb_pick0")
+
+        y_ps = []
+        for t in range(PACK):
+            bank = psum.tile([P, S], F32, name="y_ps%d" % t, tag="ya%d" % t)
+            cols = slice(P * t, P * (t + 1))
+            nc.tensor.matmul_mx(bank[:], lhsT=w_w[:, cols].bitcast(FP8X4), lhsT_scale=w_s[:, cols], rhs=xq_w[:].bitcast(FP8X4), rhs_scale=xq_s[:], start=True, stop=True)
+            y_ps.append(bank)
+
+        z = sb("z", [P, 2, PACK, HALF], F32)
+        m = sb("m", [P, PACK, S], F32)
+        bias = sb("bias", [P, PACK], F32)
+        later = {1: (cb_sb, cb_w, 1, "cb_pick1"), 2: (ca_sb, ca_w, 0, "ca_pick0"), 3: (ca_sb, ca_w, 1, "ca_pick1")}
+
+        def evac_y(t):
+            low = sb("low%d" % t, [P, 1], F32, "hold%d" % t)
+            nc.vector.tensor_scalar(y_win[t][:, :S], y_ps[t][:], 1.0, None, ALU.mult, ALU.min, accum_out=low[:])
+            nc.vector.tensor_tensor(bias[:, t : t + 1], low[:], tau_sb[:, t : t + 1], ALU.mult)
+
+        def fetch_y(t, lo, hi):
+            c0, c1 = lo // 16, hi // 16
+            nc.scalar.activation(b_win[t][:, S + lo : S + hi], y_win[t][:].indirect(n2_sb[:, c0:c1]), ACT.Copy)
+            nc.scalar.activation(a_win[t][:, S + lo : S + hi], y_win[t][:].indirect(n1_sb[:, c0:c1]), ACT.Exp, bias=bias[:, t : t + 1], scale=neg_tau[:, t : t + 1])
+
+        def make_z(t, lo, hi):
+            nc.vector.scalar_tensor_tensor(m[:, t, lo:hi], a_win[t][:, S + lo : S + hi], neg2_gs[:, t : t + 1], b_win[t][:, S + lo : S + hi], ALU.mult, ALU.mult)
+            h0, h1 = lo // HALF, hi // HALF
+            nc.vector.scalar_tensor_tensor(z[:, h0:h1, t, :], y_win[t][:, lo:hi].rearrange("p (h j) -> p h j", j=HALF), gs_sb[:, t : t + 1], m[:, t, lo:hi].rearrange("p (h j) -> p h j", j=HALF), ALU.mult, ALU.add)
+
+        def quantise_half(src, h, name, words, scales):
+            rounded = sb(name, [P, HALF, PACK], BF16)
+            nc.vector.tensor_copy(rounded[:].rearrange("p (c i) t -> p c t i", i=4), src[:, h].rearrange("p t (c i) -> p c t i", i=4))
+            cols = slice(HALF * h, HALF * (h + 1))
+            nc.vector.quantize_mx(words[:, cols].bitcast(FP8X4), scales[:, cols], rounded[:].rearrange("p j t -> p (j t)"))
+
+        z_w = sb("z_w", [P, S], U32)
+        z_s = sb("z_s", [P, S], U8)
+        evac_y(0)
+        evac_y(1)
+        fetch_y(0, 0, S)
+        pick_half(*later[1], "hold1")
+        evac_y(2)
+        evac_y(3)
+        fetch_y(1, 0, S)
+        make_z(0, 0, S)
+        pick_half(*later[2], "hold2")
+        fetch_y(2, 0, S)
+        make_z(1, 0, S)
+        pick_half(*later[3], "hold3")
+        fetch_y(3, 0, HALF)
+        fetch_y(3, HALF, S)
+        make_z(2, 0, S)
+        make_z(3, 0, HALF)
+        make_z(3, HALF, S)
+        quantise_half(z, 0, "z_bf0", z_w, z_s)
+        quantise_half(z, 1, "z_bf1", z_w, z_s)
+
+        b_ps = [psum.tile([P, S], F32, name="b_ps%d" % t, tag="b%d" % t) for t in range(PACK)]
+        for h in range(2):
+            half = slice(HALF * h, HALF * (h + 1))
+            for t in range(PACK):
+                cols = slice(P * t, P * (t + 1))
+                nc.tensor.matmul_mx(b_ps[t][:, half], lhsT=cb_w[:, cols].bitcast(FP8X4), lhsT_scale=cb_s[:, cols], rhs=z_w[:, half].bitcast(FP8X4), rhs_scale=z_s[:, half], start=True, stop=True)
+        a_ps = []
+        for t in range(PACK):
+            bank = psum.tile([P, S], F32, name="a_ps%d" % t, tag="ya%d" % t)
+            cols = slice(P * t, P * (t + 1))
+            nc.tensor.matmul_mx(bank[:], lhsT=ca_w[:, cols].bitcast(FP8X4), lhsT_scale=ca_s[:, cols], rhs=z_w[:].bitcast(FP8X4), rhs_scale=z_s[:], start=True, stop=True)
+            a_ps.append(bank)
+
+        top = sb("top", [P, PACK], F32)
+        bias2 = sb("bias2", [P, PACK], F32)
+        ea2 = sb("ea2", [P, PACK, S], F32)
+        dsq = sb("dsq", [P, PACK, S], F32)
+        inv = sb("inv", [P, PACK, S], F32)
+        a4 = sb("a4", [P, PACK, S], F32)
+        num = sb("num", [P, PACK, S], F32)
+        res = sb("res", [P, 2, PACK, HALF], F32)
+        sixteenth = sb("sixteenth", [P, 1], F32)
+        nc.vector.memset(sixteenth[:], 0.0625)
+        for t in range(PACK):
+            nc.vector.tensor_scalar(b_win[t][:, :S], b_ps[t][:], 0.0625, None, ALU.mult, ALU.max, accum_out=top[:, t : t + 1])
+            nc.vector.tensor_scalar(bias2[:, t : t + 1], top[:, t : t + 1], tau2_sb[:, t : t + 1], -1.0, ALU.mult, ALU.mult)
+            nc.scalar.activation(ea2[:, t, :], b_win[t][:].indirect(n3_sb[:]), ACT.Exp, bias=bias2[:, t : t + 1], scale=tau2_sb[:, t : t + 1])
+        for t in range(PACK):
+            nc.vector.tensor_scalar(a_win[t][:, :S], a_ps[t][:], 0.03125, None, ALU.mult)
+            nc.vector.scalar_tensor_tensor(dsq[:, t, :], ea2[:, t, :], 0.5, ea2[:, t, :], ALU.add, ALU.mult)
+
+        out_rows = out_0.rearrange("(p t) (h j) -> p h t j", t=PACK, j=HALF)
+
+        def finish(t, lo, hi):
+            h0, h1 = lo // HALF, hi // HALF
+            nc.scalar.activation(inv[:, t, lo:hi], dsq[:, t, lo:hi], ACT.Abs_reciprocal_sqrt, bias=sixteenth[:])
+            nc.vector.tensor_tensor(res[:, h0:h1, t, :], num[:, t, lo:hi].rearrange("p (h j) -> p h j", j=HALF), inv[:, t, lo:hi].rearrange("p (h j) -> p h j", j=HALF), ALU.mult)
+
+        for t in range(PACK):
+            nc.scalar.activation(a4[:, t, :], a_win[t][:].indirect(n4_sb[:]), ACT.Copy)
+            nc.vector.tensor_tensor(num[:, t, :], a_win[t][:, :S], a4[:, t, :], ALU.subtract)
+            if t < PACK - 1:
+                finish(t, 0, S)
+            else:
+                finish(t, 0, HALF)
+                finish(t, HALF, S)
+            nc.sync.dma_start(out_rows[:, :, t, :], res[:, :, t, :])
+
+        o_w = sb("o_w", [P, S], U32)
+        o_s = sb("o_s", [P, S], U8)
+        words_out = out_1[0].rearrange("p n r -> p (n r)").bitcast(I32)
+        for h in range(2):
+            quantise_half(res, h, "o_bf%d" % h, o_w, o_s)
+            cols = slice(HALF * h, HALF * (h + 1))
+            nc.sync.dma_start(words_out[:, cols], o_w[:, cols].bitcast(I32))
+        for q in range(4):
+            queue = nc.scalar if q % 2 else nc.sync
+            queue.dma_start(out_2[0][4 * q : 4 * q + 4, :].bitcast(I32), o_s[32 * q : 32 * q + 4, :].bitcast(I32))

@@ -18,6 +18,8 @@ ACT = mybir.ActivationFunctionType
 P = 128
 PACK = 4
 HALF = S // 2
+QUART = S // 4
+PIECES = ((0, HALF), (HALF, HALF + QUART), (HALF + QUART, S))
 
 
 def tile_picked_ccmpqxbebz_none_po_kernel(tc, x_words, x_scales, w1_words, w1_scales, tau, gs, tau2, offs, n1, n2, ca, cb, n3, n4, out_0, out_1, out_2):
@@ -63,12 +65,12 @@ def tile_picked_ccmpqxbebz_none_po_kernel(tc, x_words, x_scales, w1_words, w1_sc
         n4_sb = load_list("n4_sb", n4)
         tau_sb = load_column("tau_sb", tau, nc.gpsimd)
         gs_sb = load_column("gs_sb", gs, nc.gpsimd)
-        tau2_sb = load_column("tau2_sb", tau2, nc.gpsimd)
+        tau2_sb = load_column("tau2_sb", tau2, nc.sync)
 
-        y_win = [sb("y_win%d" % t, [P, 2 * S], F32) for t in range(PACK)]
+        y_win = [sb("y_win%d" % t, [P, 2 * S if t < PACK - 1 else S], F32) for t in range(PACK)]
         a_win = [sb("a_win%d" % t, [P, 2 * S], F32) for t in range(PACK)]
         b_win = [sb("b_win%d" % t, [P, 2 * S], F32) for t in range(PACK)]
-        for t in range(PACK):
+        for t in range(PACK - 1):
             nc.vector.memset(y_win[t][:, S:], 0.0)
 
         def dealt(ap):
@@ -78,8 +80,6 @@ def tile_picked_ccmpqxbebz_none_po_kernel(tc, x_words, x_scales, w1_words, w1_sc
         nc.vector.tensor_copy(xq_s[:], xs[:].indirect(offs_sb[:]))
         cb_s = sb("cb_s", [P, C], U8)
         nc.vector.tensor_copy(dealt(cb_s[:]), xs[:].indirect(cb_sb[:]))
-        ca_s = sb("ca_s", [P, C], U8)
-        nc.vector.tensor_copy(dealt(ca_s[:]), xs[:].indirect(ca_sb[:]))
         w_s = sb("w_s", [P, H], U8)
         nc.vector.tensor_copy(w_s[:].rearrange("p (t m) -> p t m", t=PACK), ws_raw[:].rearrange("p (m t) -> p t m", t=PACK))
         neg_tau = sb("neg_tau", [P, PACK], F32)
@@ -89,33 +89,25 @@ def tile_picked_ccmpqxbebz_none_po_kernel(tc, x_words, x_scales, w1_words, w1_sc
 
         xq_w = sb("xq_w", [P, S], U32)
         nc.vector.tensor_copy(xq_w[:], xw[:].indirect(offs_sb[:]))
-        w_w = sb("w_w", [P, H], U32)
+        w_w = [sb("w_w%d" % t, [P, P], U32) for t in range(PACK)]
         for t in range(PACK):
-            nc.scalar.copy(w_w[:, P * t : P * (t + 1)], ww_raw[:, t:H:PACK])
+            nc.scalar.copy(w_w[t][:], ww_raw[:, t:H:PACK])
 
-        def pick_half(lst, dst, h, name, tag=None):
-            picked = sb(name, [P, C // 2], U32, tag)
-            nc.vector.tensor_copy(picked[:], xw[:].indirect(lst[:, 16 * h : 16 * (h + 1)]))
-            nc.vector.tensor_copy(dealt(dst[:])[:, 64 * h : 64 * (h + 1), :], picked[:].rearrange("p (m t) -> p m t", t=PACK))
-
-        cb_w = sb("cb_w", [P, C], U32)
-        ca_w = sb("ca_w", [P, C], U32)
-        pick_half(cb_sb, cb_w, 0, "cb_pick0")
+        cb_w = sb("cb_w", [P, C], U32, "ws_raw")
+        nc.vector.tensor_copy(dealt(cb_w[:]), xw[:].indirect(cb_sb[:]))
 
         y_ps = []
         for t in range(PACK):
             bank = psum.tile([P, S], F32, name="y_ps%d" % t, tag="ya%d" % t)
             cols = slice(P * t, P * (t + 1))
-            nc.tensor.matmul_mx(bank[:], lhsT=w_w[:, cols].bitcast(FP8X4), lhsT_scale=w_s[:, cols], rhs=xq_w[:].bitcast(FP8X4), rhs_scale=xq_s[:], start=True, stop=True)
+            nc.tensor.matmul_mx(bank[:], lhsT=w_w[t][:].bitcast(FP8X4), lhsT_scale=w_s[:, cols], rhs=xq_w[:].bitcast(FP8X4), rhs_scale=xq_s[:], start=True, stop=True)
             y_ps.append(bank)
 
-        z = sb("z", [P, 2, PACK, HALF], F32)
-        m = sb("m", [P, PACK, S], F32)
+        z = sb("z", [P, 4, PACK, QUART], F32)
         bias = sb("bias", [P, PACK], F32)
-        later = {1: (cb_sb, cb_w, 1, "cb_pick1"), 2: (ca_sb, ca_w, 0, "ca_pick0"), 3: (ca_sb, ca_w, 1, "ca_pick1")}
 
         def evac_y(t):
-            low = sb("low%d" % t, [P, 1], F32, "hold%d" % t)
+            low = sb("low%d" % t, [P, 1], F32)
             nc.vector.tensor_scalar(y_win[t][:, :S], y_ps[t][:], 1.0, None, ALU.mult, ALU.min, accum_out=low[:])
             nc.vector.tensor_tensor(bias[:, t : t + 1], low[:], tau_sb[:, t : t + 1], ALU.mult)
 
@@ -124,38 +116,47 @@ def tile_picked_ccmpqxbebz_none_po_kernel(tc, x_words, x_scales, w1_words, w1_sc
             nc.scalar.activation(b_win[t][:, S + lo : S + hi], y_win[t][:].indirect(n2_sb[:, c0:c1]), ACT.Copy)
             nc.scalar.activation(a_win[t][:, S + lo : S + hi], y_win[t][:].indirect(n1_sb[:, c0:c1]), ACT.Exp, bias=bias[:, t : t + 1], scale=neg_tau[:, t : t + 1])
 
-        def make_z(t, lo, hi):
-            nc.vector.scalar_tensor_tensor(m[:, t, lo:hi], a_win[t][:, S + lo : S + hi], neg2_gs[:, t : t + 1], b_win[t][:, S + lo : S + hi], ALU.mult, ALU.mult)
-            h0, h1 = lo // HALF, hi // HALF
-            nc.vector.scalar_tensor_tensor(z[:, h0:h1, t, :], y_win[t][:, lo:hi].rearrange("p (h j) -> p h j", j=HALF), gs_sb[:, t : t + 1], m[:, t, lo:hi].rearrange("p (h j) -> p h j", j=HALF), ALU.mult, ALU.add)
+        def make_term(t, lo, hi, tag=None):
+            term = sb("term%d_%d" % (t, lo), [P, hi - lo], F32, tag)
+            nc.vector.scalar_tensor_tensor(term[:], a_win[t][:, S + lo : S + hi], neg2_gs[:, t : t + 1], b_win[t][:, S + lo : S + hi], ALU.mult, ALU.mult)
+            return term
 
-        def quantise_half(src, h, name, words, scales):
-            rounded = sb(name, [P, HALF, PACK], BF16)
-            nc.vector.tensor_copy(rounded[:].rearrange("p (c i) t -> p c t i", i=4), src[:, h].rearrange("p t (c i) -> p c t i", i=4))
-            cols = slice(HALF * h, HALF * (h + 1))
-            nc.vector.quantize_mx(words[:, cols].bitcast(FP8X4), scales[:, cols], rounded[:].rearrange("p j t -> p (j t)"))
+        def make_z(t, lo, hi):
+            term = make_term(t, lo, hi)
+            nc.vector.scalar_tensor_tensor(z[:, lo // QUART : hi // QUART, t, :], y_win[t][:, lo:hi].rearrange("p (h j) -> p h j", j=QUART), gs_sb[:, t : t + 1], term[:].rearrange("p (h j) -> p h j", j=QUART), ALU.mult, ALU.add)
+
+        def interleave(src, lo, hi, name, copy, rows=PACK):
+            rounded = sb(name, [P, hi - lo, PACK], BF16)
+            copy(rounded[:, :, :rows].rearrange("p (h c i) t -> p h c t i", i=4, c=QUART // 4), src[:, lo // QUART : hi // QUART, :rows].rearrange("p h t (c i) -> p h c t i", i=4))
+            return rounded
+
+        def quantise(rounded, lo, hi, words, scales):
+            nc.vector.quantize_mx(words[:, lo:hi].bitcast(FP8X4), scales[:, lo:hi], rounded[:].rearrange("p j t -> p (j t)"))
 
         z_w = sb("z_w", [P, S], U32)
         z_s = sb("z_s", [P, S], U8)
         evac_y(0)
         evac_y(1)
         fetch_y(0, 0, S)
-        pick_half(*later[1], "hold1")
+        ca_s = sb("ca_s", [P, C], U8, "low1")
+        nc.vector.tensor_copy(dealt(ca_s[:]), xs[:].indirect(ca_sb[:]))
         evac_y(2)
         evac_y(3)
         fetch_y(1, 0, S)
         make_z(0, 0, S)
-        pick_half(*later[2], "hold2")
         fetch_y(2, 0, S)
         make_z(1, 0, S)
-        pick_half(*later[3], "hold3")
-        fetch_y(3, 0, HALF)
-        fetch_y(3, HALF, S)
+        for lo, hi in PIECES:
+            fetch_y(3, lo, hi)
         make_z(2, 0, S)
-        make_z(3, 0, HALF)
-        make_z(3, HALF, S)
-        quantise_half(z, 0, "z_bf0", z_w, z_s)
-        quantise_half(z, 1, "z_bf1", z_w, z_s)
+        lo_last = PIECES[2][0]
+        z_last = interleave(z, lo_last, S, "z_bf2", nc.vector.tensor_copy, PACK - 1)
+        for n, (lo, hi) in enumerate(PIECES[:2]):
+            make_z(3, lo, hi)
+            quantise(interleave(z, lo, hi, "z_bf%d" % n, nc.vector.tensor_copy), lo, hi, z_w, z_s)
+        term = make_term(3, lo_last, S, "z_bf0")
+        nc.vector.scalar_tensor_tensor(z_last[:, :, 3], y_win[3][:, lo_last:S], gs_sb[:, 3:4], term[:], ALU.mult, ALU.add)
+        quantise(z_last, lo_last, S, z_w, z_s)
 
         b_ps = [psum.tile([P, S], F32, name="b_ps%d" % t, tag="b%d" % t) for t in range(PACK)]
         for h in range(2):
@@ -163,6 +164,22 @@ def tile_picked_ccmpqxbebz_none_po_kernel(tc, x_words, x_scales, w1_words, w1_sc
             for t in range(PACK):
                 cols = slice(P * t, P * (t + 1))
                 nc.tensor.matmul_mx(b_ps[t][:, half], lhsT=cb_w[:, cols].bitcast(FP8X4), lhsT_scale=cb_s[:, cols], rhs=z_w[:, half].bitcast(FP8X4), rhs_scale=z_s[:, half], start=True, stop=True)
+        top = [sb("top%d" % t, [P, 1], F32) for t in range(PACK)]
+        bias2 = sb("bias2", [P, PACK], F32)
+        ea2 = sb("ea2", [P, PACK, S], F32)
+        dsq = sb("dsq", [P, PACK, S], F32)
+        inv = sb("inv", [P, PACK, S], F32)
+        a4 = sb("a4", [P, PACK, S], F32)
+        num = sb("num", [P, PACK, S], F32)
+        res = sb("res", [P, 4, PACK, QUART], F32)
+        sixteenth = sb("sixteenth", [P, 1], F32)
+        nc.vector.memset(sixteenth[:], 0.0625)
+        for t in range(PACK):
+            nc.vector.tensor_scalar(b_win[t][:, :S], b_ps[t][:], 0.0625, None, ALU.mult, ALU.max, accum_out=top[t][:])
+            nc.vector.tensor_scalar(bias2[:, t : t + 1], top[t][:], tau2_sb[:, t : t + 1], -1.0, ALU.mult, ALU.mult)
+            nc.scalar.activation(ea2[:, t, :], b_win[t][:].indirect(n3_sb[:]), ACT.Exp, bias=bias2[:, t : t + 1], scale=tau2_sb[:, t : t + 1])
+        ca_w = sb("ca_w", [P, C], U32, "top3")
+        nc.vector.tensor_copy(dealt(ca_w[:]), xw[:].indirect(ca_sb[:]))
         a_ps = []
         for t in range(PACK):
             bank = psum.tile([P, S], F32, name="a_ps%d" % t, tag="ya%d" % t)
@@ -170,47 +187,37 @@ def tile_picked_ccmpqxbebz_none_po_kernel(tc, x_words, x_scales, w1_words, w1_sc
             nc.tensor.matmul_mx(bank[:], lhsT=ca_w[:, cols].bitcast(FP8X4), lhsT_scale=ca_s[:, cols], rhs=z_w[:].bitcast(FP8X4), rhs_scale=z_s[:], start=True, stop=True)
             a_ps.append(bank)
 
-        top = sb("top", [P, PACK], F32)
-        bias2 = sb("bias2", [P, PACK], F32)
-        ea2 = sb("ea2", [P, PACK, S], F32)
-        dsq = sb("dsq", [P, PACK, S], F32)
-        inv = sb("inv", [P, PACK, S], F32)
-        a4 = sb("a4", [P, PACK, S], F32)
-        num = sb("num", [P, PACK, S], F32)
-        res = sb("res", [P, 2, PACK, HALF], F32)
-        sixteenth = sb("sixteenth", [P, 1], F32)
-        nc.vector.memset(sixteenth[:], 0.0625)
         for t in range(PACK):
-            nc.vector.tensor_scalar(b_win[t][:, :S], b_ps[t][:], 0.0625, None, ALU.mult, ALU.max, accum_out=top[:, t : t + 1])
-            nc.vector.tensor_scalar(bias2[:, t : t + 1], top[:, t : t + 1], tau2_sb[:, t : t + 1], -1.0, ALU.mult, ALU.mult)
-            nc.scalar.activation(ea2[:, t, :], b_win[t][:].indirect(n3_sb[:]), ACT.Exp, bias=bias2[:, t : t + 1], scale=tau2_sb[:, t : t + 1])
+            nc.vector.scalar_tensor_tensor(dsq[:, t, :], ea2[:, t, :], 0.5, ea2[:, t, :], ALU.add, ALU.mult)
         for t in range(PACK):
             nc.vector.tensor_scalar(a_win[t][:, :S], a_ps[t][:], 0.03125, None, ALU.mult)
-            nc.vector.scalar_tensor_tensor(dsq[:, t, :], ea2[:, t, :], 0.5, ea2[:, t, :], ALU.add, ALU.mult)
 
-        out_rows = out_0.rearrange("(p t) (h j) -> p h t j", t=PACK, j=HALF)
+        out_rows = out_0.rearrange("(p t) (h j) -> p h t j", t=PACK, j=QUART)
+
+        def invert(t, lo, hi):
+            nc.scalar.activation(inv[:, t, lo:hi], dsq[:, t, lo:hi], ACT.Abs_reciprocal_sqrt, bias=sixteenth[:])
 
         def finish(t, lo, hi):
-            h0, h1 = lo // HALF, hi // HALF
-            nc.scalar.activation(inv[:, t, lo:hi], dsq[:, t, lo:hi], ACT.Abs_reciprocal_sqrt, bias=sixteenth[:])
-            nc.vector.tensor_tensor(res[:, h0:h1, t, :], num[:, t, lo:hi].rearrange("p (h j) -> p h j", j=HALF), inv[:, t, lo:hi].rearrange("p (h j) -> p h j", j=HALF), ALU.mult)
+            nc.vector.tensor_tensor(res[:, lo // QUART : hi // QUART, t, :], num[:, t, lo:hi].rearrange("p (h j) -> p h j", j=QUART), inv[:, t, lo:hi].rearrange("p (h j) -> p h j", j=QUART), ALU.mult)
 
         for t in range(PACK):
             nc.scalar.activation(a4[:, t, :], a_win[t][:].indirect(n4_sb[:]), ACT.Copy)
             nc.vector.tensor_tensor(num[:, t, :], a_win[t][:, :S], a4[:, t, :], ALU.subtract)
             if t < PACK - 1:
+                invert(t, 0, S)
                 finish(t, 0, S)
-            else:
-                finish(t, 0, HALF)
-                finish(t, HALF, S)
-            nc.sync.dma_start(out_rows[:, :, t, :], res[:, :, t, :])
+                nc.sync.dma_start(out_rows[:, :, t, :], res[:, :, t, :])
 
         o_w = sb("o_w", [P, S], U32)
         o_s = sb("o_s", [P, S], U8)
         words_out = out_1[0].rearrange("p n r -> p (n r)").bitcast(I32)
-        for h in range(2):
-            quantise_half(res, h, "o_bf%d" % h, o_w, o_s)
-            cols = slice(HALF * h, HALF * (h + 1))
+        for lo, hi in PIECES:
+            invert(3, lo, hi)
+            finish(3, lo, hi)
+        nc.sync.dma_start(out_rows[:, :, 3, :], res[:, :, 3, :])
+        for n, (lo, hi) in enumerate(PIECES):
+            quantise(interleave(res, lo, hi, "o_bf%d" % n, nc.scalar.copy if n == 1 else nc.vector.tensor_copy), lo, hi, o_w, o_s)
+        for cols in (slice(0, HALF + QUART), slice(HALF + QUART, S)):
             nc.sync.dma_start(words_out[:, cols], o_w[:, cols].bitcast(I32))
         for q in range(4):
             queue = nc.scalar if q % 2 else nc.sync

from contextlib import ExitStack

import concourse.mybir as mybir

K, T, S, H, C = 512, 2048, 256, 512, 512
FLOPS = 2 * K * S * (H + 2 * C)

F32 = mybir.dt.float32
BF16 = mybir.dt.bfloat16
I32 = mybir.dt.int32
U32 = mybir.dt.uint32
U16 = mybir.dt.uint16
U8 = mybir.dt.uint8
FP8X4 = mybir.dt.float8_e4m3fn_x4
ALU = mybir.AluOpType
ACT = mybir.ActivationFunctionType

P = 128
PACK = 4
HALF = S // 2
QUART = S // 4
PIECES = ((0, HALF), (HALF, HALF + QUART), (HALF + QUART, S))


def tile_picked_ccmpqxbebz_none_po_kernel(tc, x_words, x_scales, w1_words, w1_scales, tau, gs, tau2, offs, n1, n2, ca, cb, n3, n4, out_0, out_1, out_2):
    nc = tc.nc
    with ExitStack() as ctx:
        keep = ctx.enter_context(tc.tile_pool(name="keep", bufs=1))
        psum = ctx.enter_context(tc.psum_pool(name="psum", bufs=1))

        def sb(name, shape, dtype, tag=None):
            return keep.tile(shape, dtype, name=name, tag=tag or name, align_bytes=64)

        def load_list(name, src):
            tile = sb(name, list(src.shape), U16)
            nc.sync.dma_start(tile[:], src)
            return tile

        def load_column(name, src, queue):
            tile = sb(name, [P, PACK], F32)
            queue.dma_start(tile[:], src.rearrange("(p t) o -> p (t o)", t=PACK))
            return tile

        def load_scale_rows(tile, src, q, queue):
            rows = src[0][4 * q : 4 * q + 4, :].bitcast(I32)
            queue.dma_start(tile[32 * q : 32 * q + 32, :].bitcast(I32), rows.partition_broadcast(8))

        xs = sb("xs", [P, T], U8)
        for q in range(3):
            load_scale_rows(xs, x_scales, q, nc.scalar)
        offs_sb = load_list("offs_sb", offs)
        cb_sb = load_list("cb_sb", cb)
        ca_sb = load_list("ca_sb", ca)
        load_scale_rows(xs, x_scales, 3, nc.sync)
        xw = sb("xw", [P, T], U32)
        nc.sync.dma_start(xw[:].bitcast(I32), x_words[0].rearrange("p n r -> p (n r)").bitcast(I32))
        ws_raw = sb("ws_raw", [P, H], U8)
        for q in range(4):
            load_scale_rows(ws_raw, w1_scales, q, nc.sync)
        ww_raw = sb("ww_raw", [P, H], U32)
        nc.sync.dma_start(ww_raw[:].bitcast(I32), w1_words[0].rearrange("p n r -> p (n r)").bitcast(I32))
        n2_sb = load_list("n2_sb", n2)
        n1_sb = load_list("n1_sb", n1)
        n3_sb = load_list("n3_sb", n3)
        n4_sb = load_list("n4_sb", n4)
        tau_sb = load_column("tau_sb", tau, nc.gpsimd)
        gs_sb = load_column("gs_sb", gs, nc.gpsimd)
        tau2_sb = load_column("tau2_sb", tau2, nc.sync)

        y_win = [sb("y_win%d" % t, [P, 2 * S if t < PACK - 1 else S], F32) for t in range(PACK)]
        a_win = [sb("a_win%d" % t, [P, 2 * S], F32) for t in range(PACK)]
        b_win = [sb("b_win%d" % t, [P, 2 * S], F32) for t in range(PACK)]
        for t in range(PACK - 1):
            nc.vector.memset(y_win[t][:, S:], 0.0)

        def dealt(ap):
            return ap.rearrange("p (t m) -> p m t", t=PACK)

        xq_s = sb("xq_s", [P, S], U8)
        nc.vector.tensor_copy(xq_s[:], xs[:].indirect(offs_sb[:]))
        cb_s = sb("cb_s", [P, C], U8)
        nc.vector.tensor_copy(dealt(cb_s[:]), xs[:].indirect(cb_sb[:]))
        w_s = sb("w_s", [P, H], U8)
        nc.vector.tensor_copy(w_s[:].rearrange("p (t m) -> p t m", t=PACK), ws_raw[:].rearrange("p (m t) -> p t m", t=PACK))
        neg_tau = sb("neg_tau", [P, PACK], F32)
        nc.gpsimd.tensor_scalar(neg_tau[:], tau_sb[:], -1.0, 0.0, ALU.mult, ALU.add)
        neg2_gs = sb("neg2_gs", [P, PACK], F32)
        nc.gpsimd.tensor_scalar(neg2_gs[:], gs_sb[:], -2.0, 0.0, ALU.mult, ALU.add)

        xq_w = sb("xq_w", [P, S], U32)
        nc.vector.tensor_copy(xq_w[:], xw[:].indirect(offs_sb[:]))
        w_w = [sb("w_w%d" % t, [P, P], U32) for t in range(PACK)]
        for t in range(PACK):
            nc.scalar.copy(w_w[t][:], ww_raw[:, t:H:PACK])

        cb_w = sb("cb_w", [P, C], U32, "ws_raw")
        nc.vector.tensor_copy(dealt(cb_w[:]), xw[:].indirect(cb_sb[:]))

        y_ps = []
        for t in range(PACK):
            bank = psum.tile([P, S], F32, name="y_ps%d" % t, tag="ya%d" % t)
            cols = slice(P * t, P * (t + 1))
            nc.tensor.matmul_mx(bank[:], lhsT=w_w[t][:].bitcast(FP8X4), lhsT_scale=w_s[:, cols], rhs=xq_w[:].bitcast(FP8X4), rhs_scale=xq_s[:], start=True, stop=True)
            y_ps.append(bank)

        z = sb("z", [P, 4, PACK, QUART], F32)
        bias = sb("bias", [P, PACK], F32)

        def evac_y(t):
            low = sb("low%d" % t, [P, 1], F32)
            nc.vector.tensor_scalar(y_win[t][:, :S], y_ps[t][:], 1.0, None, ALU.mult, ALU.min, accum_out=low[:])
            nc.vector.tensor_tensor(bias[:, t : t + 1], low[:], tau_sb[:, t : t + 1], ALU.mult)

        def fetch_y(t, lo, hi):
            c0, c1 = lo // 16, hi // 16
            nc.scalar.activation(b_win[t][:, S + lo : S + hi], y_win[t][:].indirect(n2_sb[:, c0:c1]), ACT.Copy)
            nc.scalar.activation(a_win[t][:, S + lo : S + hi], y_win[t][:].indirect(n1_sb[:, c0:c1]), ACT.Exp, bias=bias[:, t : t + 1], scale=neg_tau[:, t : t + 1])

        def make_term(t, lo, hi, tag=None):
            term = sb("term%d_%d" % (t, lo), [P, hi - lo], F32, tag)
            nc.vector.scalar_tensor_tensor(term[:], a_win[t][:, S + lo : S + hi], neg2_gs[:, t : t + 1], b_win[t][:, S + lo : S + hi], ALU.mult, ALU.mult)
            return term

        def make_z(t, lo, hi):
            term = make_term(t, lo, hi)
            nc.vector.scalar_tensor_tensor(z[:, lo // QUART : hi // QUART, t, :], y_win[t][:, lo:hi].rearrange("p (h j) -> p h j", j=QUART), gs_sb[:, t : t + 1], term[:].rearrange("p (h j) -> p h j", j=QUART), ALU.mult, ALU.add)

        def interleave(src, lo, hi, name, copy, rows=PACK):
            rounded = sb(name, [P, hi - lo, PACK], BF16)
            copy(rounded[:, :, :rows].rearrange("p (h c i) t -> p h c t i", i=4, c=QUART // 4), src[:, lo // QUART : hi // QUART, :rows].rearrange("p h t (c i) -> p h c t i", i=4))
            return rounded

        def quantise(rounded, lo, hi, words, scales):
            nc.vector.quantize_mx(words[:, lo:hi].bitcast(FP8X4), scales[:, lo:hi], rounded[:].rearrange("p j t -> p (j t)"))

        z_w = sb("z_w", [P, S], U32)
        z_s = sb("z_s", [P, S], U8)
        evac_y(0)
        evac_y(1)
        fetch_y(0, 0, S)
        ca_s = sb("ca_s", [P, C], U8, "low1")
        nc.vector.tensor_copy(dealt(ca_s[:]), xs[:].indirect(ca_sb[:]))
        evac_y(2)
        evac_y(3)
        fetch_y(1, 0, S)
        make_z(0, 0, S)
        fetch_y(2, 0, S)
        make_z(1, 0, S)
        for lo, hi in PIECES:
            fetch_y(3, lo, hi)
        make_z(2, 0, S)
        lo_last = PIECES[2][0]
        z_last = interleave(z, lo_last, S, "z_bf2", nc.vector.tensor_copy, PACK - 1)
        for n, (lo, hi) in enumerate(PIECES[:2]):
            make_z(3, lo, hi)
            quantise(interleave(z, lo, hi, "z_bf%d" % n, nc.vector.tensor_copy), lo, hi, z_w, z_s)
        term = make_term(3, lo_last, S, "z_bf0")
        nc.vector.scalar_tensor_tensor(z_last[:, :, 3], y_win[3][:, lo_last:S], gs_sb[:, 3:4], term[:], ALU.mult, ALU.add)
        quantise(z_last, lo_last, S, z_w, z_s)

        b_ps = [psum.tile([P, S], F32, name="b_ps%d" % t, tag="b%d" % t) for t in range(PACK)]
        for h in range(2):
            half = slice(HALF * h, HALF * (h + 1))
            for t in range(PACK):
                cols = slice(P * t, P * (t + 1))
                nc.tensor.matmul_mx(b_ps[t][:, half], lhsT=cb_w[:, cols].bitcast(FP8X4), lhsT_scale=cb_s[:, cols], rhs=z_w[:, half].bitcast(FP8X4), rhs_scale=z_s[:, half], start=True, stop=True)
        top = [sb("top%d" % t, [P, 1], F32) for t in range(PACK)]
        bias2 = sb("bias2", [P, PACK], F32)
        ea2 = sb("ea2", [P, PACK, S], F32)
        dsq = sb("dsq", [P, PACK, S], F32)
        inv = sb("inv", [P, PACK, S], F32)
        a4 = sb("a4", [P, PACK, S], F32)
        num = sb("num", [P, PACK, S], F32)
        res = sb("res", [P, 4, PACK, QUART], F32)
        sixteenth = sb("sixteenth", [P, 1], F32)
        nc.vector.memset(sixteenth[:], 0.0625)
        for t in range(PACK):
            nc.vector.tensor_scalar(b_win[t][:, :S], b_ps[t][:], 0.0625, None, ALU.mult, ALU.max, accum_out=top[t][:])
            nc.vector.tensor_scalar(bias2[:, t : t + 1], top[t][:], tau2_sb[:, t : t + 1], -1.0, ALU.mult, ALU.mult)
            nc.scalar.activation(ea2[:, t, :], b_win[t][:].indirect(n3_sb[:]), ACT.Exp, bias=bias2[:, t : t + 1], scale=tau2_sb[:, t : t + 1])
        ca_w = sb("ca_w", [P, C], U32, "top3")
        nc.vector.tensor_copy(dealt(ca_w[:]), xw[:].indirect(ca_sb[:]))
        a_ps = []
        for t in range(PACK):
            bank = psum.tile([P, S], F32, name="a_ps%d" % t, tag="ya%d" % t)
            cols = slice(P * t, P * (t + 1))
            nc.tensor.matmul_mx(bank[:], lhsT=ca_w[:, cols].bitcast(FP8X4), lhsT_scale=ca_s[:, cols], rhs=z_w[:].bitcast(FP8X4), rhs_scale=z_s[:], start=True, stop=True)
            a_ps.append(bank)

        for t in range(PACK):
            nc.vector.scalar_tensor_tensor(dsq[:, t, :], ea2[:, t, :], 0.5, ea2[:, t, :], ALU.add, ALU.mult)
        for t in range(PACK):
            nc.vector.tensor_scalar(a_win[t][:, :S], a_ps[t][:], 0.03125, None, ALU.mult)

        out_rows = out_0.rearrange("(p t) (h j) -> p h t j", t=PACK, j=QUART)

        def invert(t, lo, hi):
            nc.scalar.activation(inv[:, t, lo:hi], dsq[:, t, lo:hi], ACT.Abs_reciprocal_sqrt, bias=sixteenth[:])

        def finish(t, lo, hi):
            nc.vector.tensor_tensor(res[:, lo // QUART : hi // QUART, t, :], num[:, t, lo:hi].rearrange("p (h j) -> p h j", j=QUART), inv[:, t, lo:hi].rearrange("p (h j) -> p h j", j=QUART), ALU.mult)

        for t in range(PACK):
            nc.scalar.activation(a4[:, t, :], a_win[t][:].indirect(n4_sb[:]), ACT.Copy)
            nc.vector.tensor_tensor(num[:, t, :], a_win[t][:, :S], a4[:, t, :], ALU.subtract)
            if t < PACK - 1:
                invert(t, 0, S)
                finish(t, 0, S)
                nc.sync.dma_start(out_rows[:, :, t, :], res[:, :, t, :])

        o_w = sb("o_w", [P, S], U32)
        o_s = sb("o_s", [P, S], U8)
        words_out = out_1[0].rearrange("p n r -> p (n r)").bitcast(I32)
        for lo, hi in PIECES:
            invert(3, lo, hi)
            finish(3, lo, hi)
        nc.sync.dma_start(out_rows[:, :, 3, :], res[:, :, 3, :])
        for n, (lo, hi) in enumerate(PIECES):
            quantise(interleave(res, lo, hi, "o_bf%d" % n, nc.scalar.copy if n == 1 else nc.vector.tensor_copy), lo, hi, o_w, o_s)
        for cols in (slice(0, HALF + QUART), slice(HALF + QUART, S)):
            nc.sync.dma_start(words_out[:, cols], o_w[:, cols].bitcast(I32))
        for q in range(4):
            queue = nc.scalar if q % 2 else nc.sync
            queue.dma_start(out_2[0][4 * q : 4 * q + 4, :].bitcast(I32), o_s[32 * q : 32 * q + 4, :].bitcast(I32))
